import numpy as np
import ml_dtypes


def mxq(x, axis, fmt="e4m3"):
    dtype, down = {"e4m3": (ml_dtypes.float8_e4m3fn, 7), "e5m2": (ml_dtypes.float8_e5m2, 14)}[fmt]
    v = np.moveaxis(np.asarray(x, np.float32).astype(ml_dtypes.bfloat16).astype(np.float64), axis, -1)
    blocks = v.reshape(v.shape[:-1] + (-1, 32))
    amax = np.abs(blocks).max(-1, keepdims=True)
    byte = np.maximum(np.where(amax > 0, np.frexp(amax)[1] - 1 + 127, 0) - down, 1)
    scale = np.exp2(byte - 127.0)
    codes = (blocks / scale).astype(np.float32).astype(dtype).astype(np.float64)
    return np.moveaxis((codes * scale).reshape(v.shape), -1, axis)


WIDE = False


def mx_kscale(k):
    if not WIDE:
        return np.ones(k)
    levels = np.array([10, -10, 5, -5, 0])
    if k % 512:
        return np.exp2(np.random.permutation(np.resize(levels, k // 32))).repeat(32)
    a = np.empty((k // 512, 16))
    for p in range(k // 512):
        a[p, :8] = np.random.permutation(np.resize(levels, 8))
        for g in range(8):
            far = levels[np.abs(levels - a[p, g]) >= 10]
            a[p, g + 8] = far[np.random.randint(len(far))]
    return np.exp2(a.ravel()).repeat(32)


def f64(x):
    return np.asarray(x).astype(np.float64)


def striped(idx):
    return np.tile(idx.reshape(-1, 16).T, (8, 1)).astype(np.uint16)


def unstriped(offs):
    return offs[:16].T.reshape(-1).astype(np.int64)


E2M1 = np.array([0.0, 0.5, 1.0, 1.5, 2.0, 3.0, 4.0, 6.0, -0.0, -0.5, -1.0, -1.5, -2.0, -3.0, -4.0, -6.0])


def pack_weight(w, fmt):
    k, n = w.shape
    w = f64(np.asarray(w, np.float32).astype(ml_dtypes.bfloat16)).reshape(k // 32, 32, n)
    amax = np.abs(w).max(1)
    if fmt == "e4m3":
        byte = np.frexp(amax)[1] - 1 + 127 - 7
    else:
        mant, ex = np.frexp(amax / 6.0)
        byte = np.where(mant > 0.5, ex, ex - 1) + 127
    byte = np.clip(np.where(amax > 0, byte, 1), 1, 254)
    scaled = (w * np.exp2(127.0 - byte)[:, None, :]).reshape(k, n).astype(np.float32)
    by_word = np.ascontiguousarray(scaled.reshape(k // 512, 128, 4, n).transpose(0, 1, 3, 2))
    if fmt == "e4m3":
        words = by_word.astype(ml_dtypes.float8_e4m3fn).view(np.uint8)
    else:
        c = by_word.astype(ml_dtypes.float4_e2m1fn).view(np.uint8) & 0xF
        words = (c[..., 0::2] | (c[..., 1::2] << 4)).reshape(k // 512, 128, 2 * n)
    return np.ascontiguousarray(words), np.ascontiguousarray(byte.astype(np.uint8).reshape(k // 512, 16, n))


def unpack_weight(words, scales, fmt):
    g, _, n = scales.shape
    words = np.ascontiguousarray(words).reshape(g, 128, n, -1)
    if fmt == "e4m3":
        vals = words.view(ml_dtypes.float8_e4m3fn).astype(np.float64)
    else:
        nib = np.empty((g, 128, n, 4), np.uint8)
        nib[..., 0::2] = words & 0xF
        nib[..., 1::2] = words >> 4
        vals = E2M1[nib]
    vals = vals * np.repeat(np.exp2(scales.astype(np.float64) - 127.0), 8, axis=1)[..., None]
    return vals.transpose(0, 1, 3, 2).reshape(g * 512, n)


def gelu(v):
    return 0.5 * v * (1.0 + np.tanh(np.sqrt(2.0 / np.pi) * (v + 0.044715 * v**3)))


K, T, S, H, K2, T2, P, N = 1024, 4096, 1024, 512, 512, 2048, 512, 384

def setup_inputs():
    n = np.random.standard_normal
    s = mx_kscale(K)[:, None]
    s2 = mx_kscale(K2)[:, None]
    u = mx_kscale(H)[:, None]
    tab_words, tab_scales = pack_weight(n((K, T)) * s, "e4m3")
    tab2_words, tab2_scales = pack_weight(n((K2, T2)) * s2, "e4m3")
    w1 = (n((K, H)) / np.sqrt(K) / s * u.T).astype(np.float32)
    w2 = (n((K, H)) / np.sqrt(K) / s * u.T).astype(np.float32)
    w3_words, w3_scales = pack_weight(n((K, H)) / np.sqrt(K) / s * u.T, "e4m3")
    w4_words, w4_scales = pack_weight(n((H, N)) / np.sqrt(H) / u, "e2m1")
    wc = (0.8 * n((K2, N)) / np.sqrt(K2) / s2).astype(np.float32)
    farm = n(N).astype(np.float32)
    return {"tab_words": tab_words, "tab_scales": tab_scales,
            "tab2_words": tab2_words, "tab2_scales": tab2_scales,
            "offs": striped(np.random.permutation(T)[:S]),
            "offs2": striped(np.random.permutation(T2)[:P]),
            "pos1": striped(np.random.permutation(S)[:P]),
            "w1": w1, "w2": w2, "w3_words": w3_words, "w3_scales": w3_scales,
            "w4_words": w4_words, "w4_scales": w4_scales, "wc": wc, "farm": farm}

def reference(tab_words, tab_scales, tab2_words, tab2_scales, offs, offs2, pos1,
              w1, w2, w3_words, w3_scales, w4_words, w4_scales, wc, farm):
    v = unpack_weight(tab_words, tab_scales, "e4m3")[:, unstriped(offs)]
    v2 = unpack_weight(tab2_words, tab2_scales, "e4m3")[:, unstriped(offs2)]
    w3 = unpack_weight(w3_words, w3_scales, "e4m3")
    w4 = unpack_weight(w4_words, w4_scales, "e2m1")
    a1 = mxq(f64(w1), 0, "e4m3").T @ v
    a2 = mxq(f64(w2), 0, "e4m3").T @ v
    a3 = w3.T @ v
    h = np.maximum(np.minimum(a1, a2), a3)
    y = w4.T @ mxq(h, 0, "e4m3")
    b = mxq(f64(wc), 0, "e4m3").T @ v2
    out = y[:, unstriped(pos1)] * np.exp(b) + f64(farm)[:, None]
    return out

from contextlib import ExitStack

import concourse.mybir as mybir

K, T, S, H, K2, T2, NP, N = 1024, 4096, 1024, 512, 512, 2048, 512, 384
FLOPS = 2 * (3 * K * H * S + H * N * S + K2 * N * NP)

F32 = mybir.dt.float32
BF16 = mybir.dt.bfloat16
I32 = mybir.dt.int32
U32 = mybir.dt.uint32
U16 = mybir.dt.uint16
U8 = mybir.dt.uint8
E4M3 = mybir.dt.float8_e4m3fn_x4
E2M1 = mybir.dt.float4_e2m1fn_x4
ALU = mybir.AluOpType
ACT = mybir.ActivationFunctionType

P = 128
PASSES = K // 512
JB = 128
BLOCKS = S // JB
NT = N // P
AHEAD = 4


def tile_list_mastitis_quarter_scores_kernel(
    tc, tab_words, tab_scales, tab2_words, tab2_scales, offs, offs2, pos1,
    w1, w2, w3_words, w3_scales, w4_words, w4_scales, wc, farm, out,
):
    nc = tc.nc
    with ExitStack() as ctx:
        keep = ctx.enter_context(tc.tile_pool(name="keep", bufs=1))
        ring = ctx.enter_context(tc.tile_pool(name="ring", bufs=2))
        psum = ctx.enter_context(tc.psum_pool(name="psum", bufs=1))

        def tile(name, shape, dtype, after=None):
            return keep.tile(shape, dtype, name=name, tag=after or name, align_bytes=64)

        def words(ap):
            return ap.rearrange("p n t -> p (n t)").bitcast(I32)

        def load_planes(name, scales, queue):
            passes, rows, width = scales.shape
            plane = tile(name, [P, width], U8)
            nc.vector.memset(plane[:].bitcast(I32), 0)
            for q in range(4):
                queue.dma_start(
                    out=plane[32 * q : 32 * q + 4 * passes, :].bitcast(I32),
                    in_=scales[:, 4 * q : 4 * q + 4, :].bitcast(I32),
                )
            return plane

        def load_rows(name, rows, after=None):
            raw = tile(name, [P, 4, rows.shape[1]], F32, after)
            nc.sync.dma_start(out=raw[:], in_=rows.rearrange("(p j) c -> p j c", j=4))
            return raw

        def load_list(name, src):
            lst = keep.tile(list(src.shape), U16, name=name)
            nc.sync.dma_start(lst[:], src)
            return lst

        def load_words(name, src, after=None):
            t = tile(name, list(src.shape), I32, after)
            nc.sync.dma_start(out=t[:], in_=src)
            return t

        tab_sc = load_planes("tab_sc", tab_scales, nc.sync)
        w3_sc_raw = load_planes("w3_sc_raw", w3_scales, nc.gpsimd)
        tab2_sc = load_planes("tab2_sc", tab2_scales, nc.gpsimd)
        w4_sc = load_planes("w4_sc", w4_scales, nc.gpsimd)
        farm_col = tile("farm_col", [P, NT], F32)
        with nc.allow_non_contiguous_dma(reason="one value of farm for each partition"):
            nc.gpsimd.dma_start(out=farm_col[:], in_=farm.rearrange("(c p) -> p c", p=P))

        idx = load_list("idx", offs)
        idx2 = load_list("idx2", offs2)
        pick = load_list("pick", pos1)
        w4 = load_words("w4", w4_words[0].bitcast(I32))
        w3_raw = [load_words("w3_raw%d" % a, words(w3_words[a])) for a in range(PASSES)]
        tab0 = load_words("tab0", words(tab_words[0]))

        def deal(copy, grouped, raw, m0):
            width = raw.shape[2] // 4
            dst = grouped[:].rearrange("p (t m j) -> p m j t", t=4, j=4)[:, m0 : m0 + width]
            copy(out=dst, in_=raw[:].rearrange("p j (m t) -> p m j t", t=4))

        def quantise(name, grouped):
            width = grouped.shape[1] // 4
            codes = tile(name + "_codes", [P, width], U32)
            plane = tile(name + "_plane", [P, width], U8)
            nc.vector.quantize_mx(out=codes[:].bitcast(E4M3), scales=plane[:], in_=grouped[:])
            return codes, plane

        def gather(name, window, lst, c0, c1, dtype, after=None):
            got = tile(name, [P, 16 * (c1 - c0)], dtype, after)
            nc.vector.tensor_copy(got[:], window[:].bitcast(dtype).indirect(lst[:, c0:c1]))
            return got

        w3 = tile("w3", [P, PASSES, H], I32)
        for a in range(PASSES):
            nc.vector.tensor_copy(
                out=w3[:, a, :].rearrange("p (t m) -> p m t", t=4),
                in_=w3_raw[a][:].rearrange("p (m t) -> p m t", t=4),
            )
        w1_raw0 = load_rows("w1_raw0", w1[0:512, :], "w3_raw0")
        tab1 = load_words("tab1", words(tab_words[1]), "w3_raw1")

        v0 = gather("v0", tab0, idx, 0, 64, U32)
        v_sc = gather("v_sc", tab_sc, idx, 0, 64, U8)
        w1_raw1 = load_rows("w1_raw1", w1[512:1024, :], "tab_sc")
        w2_raw0 = load_rows("w2_raw0", w2[0:512, :], "tab0")

        grouped = tile("w1_bf0", [P, 4 * H], BF16)
        deal(nc.vector.tensor_copy, grouped, w1_raw0, 0)
        w1q = [quantise("w1_0", grouped)]
        w3_sc = tile("w3_sc", [P, H], U8, "w1_bf0")
        nc.vector.tensor_copy(
            out=w3_sc[:].rearrange("p (t m) -> p t m", t=4),
            in_=w3_sc_raw[:].rearrange("p (m t) -> p t m", t=4),
        )
        w2_raw1 = [
            load_rows("w2_raw1_%d" % u, w2[512:1024, 256 * u : 256 * (u + 1)], after)
            for u, after in enumerate(("w3_raw0", "w3_sc_raw"))
        ]
        v1 = [gather("v1_%d" % u, tab1, idx, 32 * u, 32 * (u + 1), U32) for u in range(2)]

        def moving(a, b):
            if a == 0:
                codes = v0[:, JB * b : JB * (b + 1)]
            else:
                codes = v1[b // 4][:, JB * (b % 4) : JB * (b % 4 + 1)]
            return codes.bitcast(E4M3), v_sc[4 * a : P, JB * b : JB * (b + 1)]

        def product(tag, bufs, weight, b):
            bank = psum.tile([P, 4, JB], F32, name=tag, tag=tag, bufs=bufs)
            for t in range(4):
                for a in range(PASSES):
                    codes, plane = weight(a, slice(P * t, P * (t + 1)))
                    rhs, rhs_scale = moving(a, b)
                    nc.tensor.matmul_mx(
                        out=bank[:, t, :], lhsT=codes.bitcast(E4M3), lhsT_scale=plane,
                        rhs=rhs, rhs_scale=rhs_scale, start=(a == 0), stop=(a == PASSES - 1),
                    )
            return bank[:].rearrange("p t j -> p j t")

        def held_product(name, weight, b):
            acc = product("side", 4, weight, b)
            held = tile("%s_%d" % (name, b), [P, JB, 4], F32)
            nc.scalar.copy(out=held[:], in_=acc)
            return held

        a3 = [
            held_product("a3", lambda a, cols: (w3[:, a, cols], w3_sc[4 * a : P, cols]), b) for b in range(BLOCKS)
        ]

        grouped = tile("w1_bf1", [P, 4 * H], BF16, "w3_raw1")
        deal(nc.vector.tensor_copy, grouped, w1_raw1, 0)
        w1q.append(quantise("w1_1", grouped))
        wc_raw = load_rows("wc_raw", wc, "tab_sc")

        def first_reading(b):
            return held_product("a1", lambda a, cols: (w1q[a][0][:, cols], w1q[a][1][:, cols]), b)

        a1 = [first_reading(b) for b in range(AHEAD)]

        grouped = tile("w2_bf0", [P, 4 * H], BF16, "w3_raw1")
        deal(nc.vector.tensor_copy, grouped, w2_raw0, 0)
        w2q = [quantise("w2_0", grouped)]
        grouped = tile("w2_bf1", [P, 4 * H], BF16, "w3_raw1")
        for u in range(2):
            deal(nc.vector.tensor_copy, grouped, w2_raw1[u], 64 * u)
        w2q.append(quantise("w2_1", grouped))
        tab2 = load_words("tab2", words(tab2_words[0]), "w3_raw0")

        y = [tile("y%d" % n, [P, S], F32) for n in range(NT)]
        w4_u8 = w4[:].bitcast(U8)

        def second_stage(h_bf, j0):
            codes, plane = quantise("h%d" % j0, h_bf)
            width = codes.shape[1]
            for n in range(NT):
                bank = psum.tile([P, 512], F32, name="side", tag="side", bufs=4)
                nc.tensor.matmul_mx(
                    out=bank[:, 0:width], lhsT=w4_u8[:, 2 * P * n : 2 * P * (n + 1)].bitcast(E2M1),
                    lhsT_scale=w4_sc[:, P * n : P * (n + 1)], rhs=codes[:].bitcast(E4M3), rhs_scale=plane[:],
                    start=True, stop=True,
                )
                nc.scalar.copy(out=y[n][:, j0 : j0 + width], in_=bank[:, 0:width])

        def cultures():
            v2 = gather("v2", tab2, idx2, 0, 32, U32)
            v2_sc = gather("v2_sc", tab2_sc, idx2, 0, 32, U8, "w3_raw1")
            grouped = tile("wc_bf", [P, 4 * N], BF16, "w1_1_codes")
            nc.scalar.copy(
                out=grouped[:].rearrange("p (c i j) -> p c j i", i=4, j=4),
                in_=wc_raw[:].rearrange("p j (c i) -> p c j i", i=4),
            )
            codes, plane = quantise("wc", grouped)
            factors = []
            for n in range(NT):
                bank = psum.tile([P, 512], F32, name="side", tag="side", bufs=4)
                cols = slice(P * n, P * (n + 1))
                nc.tensor.matmul_mx(
                    out=bank[:], lhsT=codes[:, cols].bitcast(E4M3), lhsT_scale=plane[:, cols],
                    rhs=v2[:].bitcast(E4M3), rhs_scale=v2_sc[:], start=True, stop=True,
                )
                factor = tile("factor%d" % n, [P, NP], F32)
                nc.scalar.activation(out=factor[:], in_=bank[:], func=ACT.Exp)
                factors.append(factor)
            return factors

        pending = None
        for pair in range(BLOCKS // 2):
            h_bf = tile("h_bf%d" % pair, [P, 2 * JB * 4], BF16)
            lows = []
            for u in range(2):
                b = 2 * pair + u
                acc2 = product("a2", 4, lambda a, cols: (w2q[a][0][:, cols], w2q[a][1][:, cols]), b)
                low = ring.tile([P, JB, 4], F32, name="low")
                nc.vector.tensor_tensor(out=low[:], in0=acc2, in1=a1[b][:], op=ALU.min)
                lows.append(low)
                if b + AHEAD < BLOCKS:
                    a1.append(first_reading(b + AHEAD))
            if pending is not None:
                second_stage(*pending)
            for u in range(2):
                b = 2 * pair + u
                dst = h_bf[:, 4 * JB * u : 4 * JB * (u + 1)].rearrange("p (j t) -> p j t", t=4)
                nc.vector.tensor_tensor(out=dst, in0=lows[u][:], in1=a3[b][:], op=ALU.max)
            pending = (h_bf, 2 * JB * pair)
            if pair == 2:
                factors = cultures()
        second_stage(*pending)

        for n in range(NT):
            scaled = tile("scaled%d" % n, [P, NP], F32)
            nc.vector.tensor_tensor(scaled[:], y[n][:].indirect(pick[:]), factors[n][:], ALU.mult)
            result = tile("result%d" % n, [P, NP], F32)
            nc.scalar.activation(out=result[:], in_=scaled[:], func=ACT.Identity, bias=farm_col[:, n : n + 1])
            nc.sync.dma_start(out=out[P * n : P * (n + 1), :], in_=result[:])
